import numpy as np
import ml_dtypes


def mxq(x, axis, fmt="e4m3"):
    dtype, down = {"e4m3": (ml_dtypes.float8_e4m3fn, 7), "e5m2": (ml_dtypes.float8_e5m2, 14)}[fmt]
    v = np.moveaxis(np.asarray(x, np.float32).astype(ml_dtypes.bfloat16).astype(np.float64), axis, -1)
    blocks = v.reshape(v.shape[:-1] + (-1, 32))
    amax = np.abs(blocks).max(-1, keepdims=True)
    byte = np.maximum(np.where(amax > 0, np.frexp(amax)[1] - 1 + 127, 0) - down, 1)
    scale = np.exp2(byte - 127.0)
    codes = (blocks / scale).astype(np.float32).astype(dtype).astype(np.float64)
    return np.moveaxis((codes * scale).reshape(v.shape), -1, axis)


WIDE = False


def mx_kscale(k):
    if not WIDE:
        return np.ones(k)
    levels = np.array([10, -10, 5, -5, 0])
    if k % 512:
        return np.exp2(np.random.permutation(np.resize(levels, k // 32))).repeat(32)
    a = np.empty((k // 512, 16))
    for p in range(k // 512):
        a[p, :8] = np.random.permutation(np.resize(levels, 8))
        for g in range(8):
            far = levels[np.abs(levels - a[p, g]) >= 10]
            a[p, g + 8] = far[np.random.randint(len(far))]
    return np.exp2(a.ravel()).repeat(32)


def f64(x):
    return np.asarray(x).astype(np.float64)


def striped8(idx):
    return np.asarray(idx).reshape(8, -1, 16).transpose(0, 2, 1).reshape(128, -1).astype(np.uint16)


def unstriped8(offs):
    return offs.reshape(8, 16, -1).transpose(0, 2, 1).reshape(8, -1).astype(np.int64)


def pick8(x, idx, run):
    r = np.arange(len(x))
    return x[r[:, None], idx[r % (8 * run) // run]]


E2M1 = np.array([0.0, 0.5, 1.0, 1.5, 2.0, 3.0, 4.0, 6.0, -0.0, -0.5, -1.0, -1.5, -2.0, -3.0, -4.0, -6.0])


def pack_weight(w, fmt):
    k, n = w.shape
    w = f64(np.asarray(w, np.float32).astype(ml_dtypes.bfloat16)).reshape(k // 32, 32, n)
    amax = np.abs(w).max(1)
    if fmt == "e4m3":
        byte = np.frexp(amax)[1] - 1 + 127 - 7
    else:
        mant, ex = np.frexp(amax / 6.0)
        byte = np.where(mant > 0.5, ex, ex - 1) + 127
    byte = np.clip(np.where(amax > 0, byte, 1), 1, 254)
    scaled = (w * np.exp2(127.0 - byte)[:, None, :]).reshape(k, n).astype(np.float32)
    by_word = np.ascontiguousarray(scaled.reshape(k // 512, 128, 4, n).transpose(0, 1, 3, 2))
    if fmt == "e4m3":
        words = by_word.astype(ml_dtypes.float8_e4m3fn).view(np.uint8)
    else:
        c = by_word.astype(ml_dtypes.float4_e2m1fn).view(np.uint8) & 0xF
        words = (c[..., 0::2] | (c[..., 1::2] << 4)).reshape(k // 512, 128, 2 * n)
    return np.ascontiguousarray(words), np.ascontiguousarray(byte.astype(np.uint8).reshape(k // 512, 16, n))


def unpack_weight(words, scales, fmt):
    g, _, n = scales.shape
    words = np.ascontiguousarray(words).reshape(g, 128, n, -1)
    if fmt == "e4m3":
        vals = words.view(ml_dtypes.float8_e4m3fn).astype(np.float64)
    else:
        nib = np.empty((g, 128, n, 4), np.uint8)
        nib[..., 0::2] = words & 0xF
        nib[..., 1::2] = words >> 4
        vals = E2M1[nib]
    vals = vals * np.repeat(np.exp2(scales.astype(np.float64) - 127.0), 8, axis=1)[..., None]
    return vals.transpose(0, 1, 3, 2).reshape(g * 512, n)


D, T, Z, I, Q = 512, 1024, 1024, 512, 128


def setup_inputs():
    n = np.random.standard_normal
    idx = np.stack([np.random.permutation(T)[:I] for _ in range(8)])
    idx2 = np.stack([np.random.permutation(Z)[:I] for _ in range(8)])
    idx3 = np.stack([np.random.permutation(Z)[:I] for _ in range(8)])
    fd = mx_kscale(D)
    keysp = pack_weight(n((D, T)) / fd[:, None], "e4m3")
    tagsp = pack_weight(n((D, T)) / fd[:, None], "e2m1")
    return {
        "query": (n((D, Q)) * 0.75 / np.sqrt(D) * fd[:, None]).astype(np.float32),
        "query2": (n((D, Q)) * 0.75 / np.sqrt(D) * fd[:, None]).astype(np.float32),
        "keys_words": keysp[0],
        "keys_scales": keysp[1],
        "tags_words": tagsp[0],
        "tags_scales": tagsp[1],
        "old": (1.0 * n((Q, Z))).astype(np.float32),
        "lam": (np.random.uniform(0.5, 1.5, (Q, 1))).astype(np.float32),
        "offs": striped8(idx),
        "offs2": striped8(idx2),
        "offs3": striped8(idx3),
    }


def reference(query, query2, keys_words, keys_scales, tags_words, tags_scales, old, lam, offs, offs2, offs3):
    idx = unstriped8(offs)
    idx2 = unstriped8(offs2)
    idx3 = unstriped8(offs3)
    keysu = unpack_weight(keys_words, keys_scales, "e4m3")
    tagsu = unpack_weight(tags_words, tags_scales, "e2m1")
    queryq = mxq(f64(query), 0, "e4m3")
    query2q = mxq(f64(query2), 0, "e4m3")
    a = queryq.T @ keysu + query2q.T @ tagsu
    w = pick8(a, idx, 16) - pick8(f64(old), idx2, 16)
    f1 = np.zeros((Q, Z))
    f1[np.arange(Q)[:, None], idx2[np.arange(Q) % 128 // 16]] = w
    cc = f64(old) + f1 * f64(lam)
    y = pick8(cc, idx3, 16)
    return y

@@ -1,0 +1,117 @@
+from contextlib import ExitStack
+
+import concourse.mybir as mybir
+
+D, T, Z, I, Q = 512, 1024, 1024, 512, 128
+FLOPS = 2 * 2 * D * T * Q
+
+F32 = mybir.dt.float32
+BF16 = mybir.dt.bfloat16
+I32 = mybir.dt.int32
+U32 = mybir.dt.uint32
+U16 = mybir.dt.uint16
+U8 = mybir.dt.uint8
+FP8X4 = mybir.dt.float8_e4m3fn_x4
+FP4X4 = mybir.dt.float4_e2m1fn_x4
+ADD = mybir.AluOpType.add
+MULT = mybir.AluOpType.mult
+COPY = mybir.ActivationFunctionType.Copy
+
+P = 128
+PACK = 4
+BANKS = 4
+BANK_T = T // BANKS
+HALF_T = T // 2
+HALF_I = I // 2
+HALF_COLS = HALF_I // 16
+
+
+def tile_attend_rebased_parts_kernel(tc, query, query2, keys_words, keys_scales, tags_words, tags_scales,
+                                      old, lam, offs, offs2, offs3, out):
+    nc = tc.nc
+    with ExitStack() as ctx:
+        pool = ctx.enter_context(tc.tile_pool(name="held", bufs=1))
+        psum = ctx.enter_context(tc.psum_pool(name="psum", bufs=1))
+
+        list_a = pool.tile([P, I // 16], U16, name="list_a")
+        list_old = pool.tile([P, I // 16], U16, name="list_old")
+        list_cc = pool.tile([P, I // 16], U16, name="list_cc")
+        tag_plane = pool.tile([P, T], U8, name="tag_plane", align_bytes=64)
+        key_plane = pool.tile([P, T], U8, name="key_plane", align_bytes=64)
+        tag_codes = pool.tile([P, 2 * T], U8, name="tag_codes", align_bytes=64)
+        key_codes = [pool.tile([P, HALF_T], U32, name="key_codes%d" % h, align_bytes=64) for h in range(2)]
+        raw = [pool.tile([P, PACK, Q], F32, name="raw%d" % j) for j in range(2)]
+        grouped = [pool.tile([P, Q, PACK], BF16, name="grouped%d" % j, align_bytes=64) for j in range(2)]
+        q_codes = [pool.tile([P, Q], U32, name="q_codes%d" % j, align_bytes=64) for j in range(2)]
+        q_plane = [pool.tile([P, Q], U8, name="q_plane%d" % j, align_bytes=64) for j in range(2)]
+        old_sb = pool.tile([P, Z], F32, name="old_sb")
+        lam_sb = pool.tile([P, 1], F32, name="lam_sb")
+        a_sb = pool.tile([P, T], F32, name="a_sb")
+        f1 = pool.tile([P, Z], F32, name="f1")
+        cc = pool.tile([P, Z], F32, name="cc")
+        a_pick = [pool.tile([P, HALF_I], F32, name="a_pick%d" % h) for h in range(2)]
+        old_neg = [pool.tile([P, HALF_I], F32, name="old_neg%d" % h) for h in range(2)]
+        y = [pool.tile([P, HALF_I], F32, name="y%d" % h) for h in range(2)]
+        banks = [psum.tile([P, BANK_T], F32, name="bank%d" % b) for b in range(BANKS)]
+
+        nc.vector.memset(tag_plane[:].bitcast(I32), 0)
+        nc.vector.memset(key_plane[:].bitcast(I32), 0)
+        nc.vector.memset(f1[:], 0.0)
+
+        def load_query(j, src):
+            nc.sync.dma_start(out=raw[j][:], in_=src.rearrange("(p r) q -> p r q", r=PACK))
+
+        def load_plane(plane, scales):
+            for r in range(4):
+                nc.sync.dma_start(out=plane[r:P:32, :].bitcast(I32), in_=scales[0, r:16:4, :].bitcast(I32))
+
+        def load_keys(h):
+            words = keys_words[0].rearrange("p n r -> p (n r)")
+            nc.sync.dma_start(out=key_codes[h][:].bitcast(I32),
+                              in_=words[:, PACK * HALF_T * h:PACK * HALF_T * (h + 1)].bitcast(I32))
+
+        load_query(1, query2)
+        load_plane(tag_plane, tags_scales)
+        nc.sync.dma_start(out=tag_codes[:].bitcast(I32), in_=tags_words[0].bitcast(I32))
+        load_query(0, query)
+        load_keys(0)
+        load_plane(key_plane, keys_scales)
+        load_keys(1)
+        nc.sync.dma_start(out=old_sb[:], in_=old)
+        nc.sync.dma_start(list_old[:], offs2)
+        nc.sync.dma_start(list_a[:], offs)
+        nc.sync.dma_start(list_cc[:], offs3)
+        nc.sync.dma_start(out=lam_sb[:], in_=lam)
+
+        for j in (1, 0):
+            nc.vector.tensor_copy(out=grouped[j][:], in_=raw[j][:].rearrange("p r q -> p q r"))
+            nc.vector.quantize_mx(out=q_codes[j][:].bitcast(FP8X4), scales=q_plane[j][:],
+                                  in_=grouped[j][:].rearrange("p q r -> p (q r)"))
+
+        for b in range(BANKS):
+            nc.tensor.matmul_mx(out=banks[b][:], lhsT=q_codes[1][:].bitcast(FP8X4), lhsT_scale=q_plane[1][:],
+                                rhs=tag_codes[:, 2 * BANK_T * b:2 * BANK_T * (b + 1)].bitcast(FP4X4),
+                                rhs_scale=tag_plane[:, BANK_T * b:BANK_T * (b + 1)], start=True, stop=False)
+        for b in range(BANKS):
+            h, c = divmod(BANK_T * b, HALF_T)
+            nc.tensor.matmul_mx(out=banks[b][:], lhsT=q_codes[0][:].bitcast(FP8X4), lhsT_scale=q_plane[0][:],
+                                rhs=key_codes[h][:, c:c + BANK_T].bitcast(FP8X4),
+                                rhs_scale=key_plane[:, BANK_T * b:BANK_T * (b + 1)], start=False, stop=True)
+            nc.vector.tensor_copy(out=a_sb[:, BANK_T * b:BANK_T * (b + 1)], in_=banks[b][:])
+
+        def half(lst, h):
+            return lst[:, HALF_COLS * h:HALF_COLS * (h + 1)]
+
+        nc.scalar.activation(old_neg[0][:], old_sb[:].indirect(half(list_old, 0)), COPY, scale=-1.0)
+        nc.vector.tensor_copy(a_pick[0][:], a_sb[:].indirect(half(list_a, 0)))
+        nc.scalar.activation(old_neg[1][:], old_sb[:].indirect(half(list_old, 1)), COPY, scale=-1.0)
+        nc.scalar.activation(a_pick[1][:], a_sb[:].indirect(half(list_a, 1)), COPY)
+        for h in range(2):
+            nc.vector.tensor_tensor(f1[:].indirect(half(list_old, h)), a_pick[h][:], old_neg[h][:], ADD)
+
+        nc.vector.scalar_tensor_tensor(cc[:], f1[:], lam_sb[:], old_sb[:], MULT, ADD)
+
+        nc.vector.tensor_copy(y[0][:], cc[:].indirect(half(list_cc, 0)))
+        nc.scalar.activation(y[1][:], cc[:].indirect(half(list_cc, 1)), COPY)
+        nc.sync.dma_start(out=out[:, 0:HALF_I], in_=y[0][:])
+        nc.scalar.dma_start(out=out[:, HALF_I:I], in_=y[1][:])

@@ -54,6 +54,11 @@ def tile_attend_rebased_parts_kernel(tc, query, query2, keys_words, keys_scales,
         y = [pool.tile([P, HALF_I], F32, name="y%d" % h) for h in range(2)]
         banks = [psum.tile([P, BANK_T], F32, name="bank%d" % b) for b in range(BANKS)]
 
+        warm_in = pool.tile([P, 1], F32, name="warm_in")
+        warm_out = pool.tile([P, 1], F32, name="warm_out")
+        nc.gpsimd.memset(warm_in[:], 0.0)
+        nc.scalar.activation(warm_out[:], warm_in[:], COPY)
+
         nc.vector.memset(tag_plane[:].bitcast(I32), 0)
         nc.vector.memset(key_plane[:].bitcast(I32), 0)
         nc.vector.memset(f1[:], 0.0)

@@ -19,9 +19,7 @@ COPY = mybir.ActivationFunctionType.Copy
 
 P = 128
 PACK = 4
-BANKS = 4
-BANK_T = T // BANKS
-HALF_T = T // 2
+BANK_WIDTHS = (256, 256, 256, 128, 128)
 HALF_I = I // 2
 HALF_COLS = HALF_I // 16
 
@@ -39,7 +37,7 @@ def tile_attend_rebased_parts_kernel(tc, query, query2, keys_words, keys_scales,
         tag_plane = pool.tile([P, T], U8, name="tag_plane", align_bytes=64)
         key_plane = pool.tile([P, T], U8, name="key_plane", align_bytes=64)
         tag_codes = pool.tile([P, 2 * T], U8, name="tag_codes", align_bytes=64)
-        key_codes = [pool.tile([P, HALF_T], U32, name="key_codes%d" % h, align_bytes=64) for h in range(2)]
+        key_codes = pool.tile([P, T], U32, name="key_codes", align_bytes=64)
         raw = [pool.tile([P, PACK, Q], F32, name="raw%d" % j) for j in range(2)]
         grouped = [pool.tile([P, Q, PACK], BF16, name="grouped%d" % j, align_bytes=64) for j in range(2)]
         q_codes = [pool.tile([P, Q], U32, name="q_codes%d" % j, align_bytes=64) for j in range(2)]
@@ -52,7 +50,8 @@ def tile_attend_rebased_parts_kernel(tc, query, query2, keys_words, keys_scales,
         a_pick = [pool.tile([P, HALF_I], F32, name="a_pick%d" % h) for h in range(2)]
         old_neg = [pool.tile([P, HALF_I], F32, name="old_neg%d" % h) for h in range(2)]
         y = [pool.tile([P, HALF_I], F32, name="y%d" % h) for h in range(2)]
-        banks = [psum.tile([P, BANK_T], F32, name="bank%d" % b) for b in range(BANKS)]
+        banks = [psum.tile([P, n], F32, name="bank%d" % b) for b, n in enumerate(BANK_WIDTHS)]
+        starts = [sum(BANK_WIDTHS[:b]) for b in range(len(BANK_WIDTHS))]
 
         warm_in = pool.tile([P, 1], F32, name="warm_in")
         warm_out = pool.tile([P, 1], F32, name="warm_out")
@@ -70,21 +69,16 @@ def tile_attend_rebased_parts_kernel(tc, query, query2, keys_words, keys_scales,
             for r in range(4):
                 nc.sync.dma_start(out=plane[r:P:32, :].bitcast(I32), in_=scales[0, r:16:4, :].bitcast(I32))
 
-        def load_keys(h):
-            words = keys_words[0].rearrange("p n r -> p (n r)")
-            nc.sync.dma_start(out=key_codes[h][:].bitcast(I32),
-                              in_=words[:, PACK * HALF_T * h:PACK * HALF_T * (h + 1)].bitcast(I32))
-
         load_query(1, query2)
-        load_plane(tag_plane, tags_scales)
         nc.sync.dma_start(out=tag_codes[:].bitcast(I32), in_=tags_words[0].bitcast(I32))
+        load_plane(tag_plane, tags_scales)
         load_query(0, query)
-        load_keys(0)
+        nc.sync.dma_start(out=key_codes[:].bitcast(I32),
+                          in_=keys_words[0].rearrange("p n r -> p (n r)").bitcast(I32))
         load_plane(key_plane, keys_scales)
-        load_keys(1)
-        nc.sync.dma_start(out=old_sb[:], in_=old)
         nc.sync.dma_start(list_old[:], offs2)
         nc.sync.dma_start(list_a[:], offs)
+        nc.sync.dma_start(out=old_sb[:], in_=old)
         nc.sync.dma_start(list_cc[:], offs3)
         nc.sync.dma_start(out=lam_sb[:], in_=lam)
 
@@ -93,24 +87,26 @@ def tile_attend_rebased_parts_kernel(tc, query, query2, keys_words, keys_scales,
             nc.vector.quantize_mx(out=q_codes[j][:].bitcast(FP8X4), scales=q_plane[j][:],
                                   in_=grouped[j][:].rearrange("p q r -> p (q r)"))
 
-        for b in range(BANKS):
-            nc.tensor.matmul_mx(out=banks[b][:], lhsT=q_codes[1][:].bitcast(FP8X4), lhsT_scale=q_plane[1][:],
-                                rhs=tag_codes[:, 2 * BANK_T * b:2 * BANK_T * (b + 1)].bitcast(FP4X4),
-                                rhs_scale=tag_plane[:, BANK_T * b:BANK_T * (b + 1)], start=True, stop=False)
-        for b in range(BANKS):
-            h, c = divmod(BANK_T * b, HALF_T)
-            nc.tensor.matmul_mx(out=banks[b][:], lhsT=q_codes[0][:].bitcast(FP8X4), lhsT_scale=q_plane[0][:],
-                                rhs=key_codes[h][:, c:c + BANK_T].bitcast(FP8X4),
-                                rhs_scale=key_plane[:, BANK_T * b:BANK_T * (b + 1)], start=False, stop=True)
-            nc.vector.tensor_copy(out=a_sb[:, BANK_T * b:BANK_T * (b + 1)], in_=banks[b][:])
+        for bank, t0, n in zip(banks, starts, BANK_WIDTHS):
+            nc.tensor.matmul_mx(out=bank[:], lhsT=q_codes[1][:].bitcast(FP8X4), lhsT_scale=q_plane[1][:],
+                                rhs=tag_codes[:, 2 * t0:2 * (t0 + n)].bitcast(FP4X4),
+                                rhs_scale=tag_plane[:, t0:t0 + n], start=True, stop=False)
+        for b, (bank, t0, n) in enumerate(zip(banks, starts, BANK_WIDTHS)):
+            nc.tensor.matmul_mx(out=bank[:], lhsT=q_codes[0][:].bitcast(FP8X4), lhsT_scale=q_plane[0][:],
+                                rhs=key_codes[:, t0:t0 + n].bitcast(FP8X4),
+                                rhs_scale=key_plane[:, t0:t0 + n], start=False, stop=True)
+            if b % 2 == 0:
+                nc.vector.tensor_copy(out=a_sb[:, t0:t0 + n], in_=bank[:])
+            else:
+                nc.scalar.copy(out=a_sb[:, t0:t0 + n], in_=bank[:])
 
         def half(lst, h):
             return lst[:, HALF_COLS * h:HALF_COLS * (h + 1)]
 
-        nc.scalar.activation(old_neg[0][:], old_sb[:].indirect(half(list_old, 0)), COPY, scale=-1.0)
-        nc.vector.tensor_copy(a_pick[0][:], a_sb[:].indirect(half(list_a, 0)))
-        nc.scalar.activation(old_neg[1][:], old_sb[:].indirect(half(list_old, 1)), COPY, scale=-1.0)
+        nc.scalar.activation(a_pick[0][:], a_sb[:].indirect(half(list_a, 0)), COPY)
+        nc.vector.tensor_scalar(old_neg[0][:], old_sb[:].indirect(half(list_old, 0)), -1.0, 0.0, MULT, ADD)
         nc.scalar.activation(a_pick[1][:], a_sb[:].indirect(half(list_a, 1)), COPY)
+        nc.scalar.activation(old_neg[1][:], old_sb[:].indirect(half(list_old, 1)), COPY, scale=-1.0)
         for h in range(2):
             nc.vector.tensor_tensor(f1[:].indirect(half(list_old, h)), a_pick[h][:], old_neg[h][:], ADD)
 

from contextlib import ExitStack

import concourse.mybir as mybir

D, T, Z, I, Q = 512, 1024, 1024, 512, 128
FLOPS = 2 * 2 * D * T * Q

F32 = mybir.dt.float32
BF16 = mybir.dt.bfloat16
I32 = mybir.dt.int32
U32 = mybir.dt.uint32
U16 = mybir.dt.uint16
U8 = mybir.dt.uint8
FP8X4 = mybir.dt.float8_e4m3fn_x4
FP4X4 = mybir.dt.float4_e2m1fn_x4
ADD = mybir.AluOpType.add
MULT = mybir.AluOpType.mult
COPY = mybir.ActivationFunctionType.Copy

P = 128
PACK = 4
BANK_WIDTHS = (256, 256, 256, 128, 128)
HALF_I = I // 2
HALF_COLS = HALF_I // 16


def tile_attend_rebased_parts_kernel(tc, query, query2, keys_words, keys_scales, tags_words, tags_scales,
                                      old, lam, offs, offs2, offs3, out):
    nc = tc.nc
    with ExitStack() as ctx:
        pool = ctx.enter_context(tc.tile_pool(name="held", bufs=1))
        psum = ctx.enter_context(tc.psum_pool(name="psum", bufs=1))

        list_a = pool.tile([P, I // 16], U16, name="list_a")
        list_old = pool.tile([P, I // 16], U16, name="list_old")
        list_cc = pool.tile([P, I // 16], U16, name="list_cc")
        tag_plane = pool.tile([P, T], U8, name="tag_plane", align_bytes=64)
        key_plane = pool.tile([P, T], U8, name="key_plane", align_bytes=64)
        tag_codes = pool.tile([P, 2 * T], U8, name="tag_codes", align_bytes=64)
        key_codes = pool.tile([P, T], U32, name="key_codes", align_bytes=64)
        raw = [pool.tile([P, PACK, Q], F32, name="raw%d" % j) for j in range(2)]
        grouped = [pool.tile([P, Q, PACK], BF16, name="grouped%d" % j, align_bytes=64) for j in range(2)]
        q_codes = [pool.tile([P, Q], U32, name="q_codes%d" % j, align_bytes=64) for j in range(2)]
        q_plane = [pool.tile([P, Q], U8, name="q_plane%d" % j, align_bytes=64) for j in range(2)]
        old_sb = pool.tile([P, Z], F32, name="old_sb")
        lam_sb = pool.tile([P, 1], F32, name="lam_sb")
        a_sb = pool.tile([P, T], F32, name="a_sb")
        f1 = pool.tile([P, Z], F32, name="f1")
        cc = pool.tile([P, Z], F32, name="cc")
        a_pick = [pool.tile([P, HALF_I], F32, name="a_pick%d" % h) for h in range(2)]
        old_neg = [pool.tile([P, HALF_I], F32, name="old_neg%d" % h) for h in range(2)]
        y = [pool.tile([P, HALF_I], F32, name="y%d" % h) for h in range(2)]
        banks = [psum.tile([P, n], F32, name="bank%d" % b) for b, n in enumerate(BANK_WIDTHS)]
        starts = [sum(BANK_WIDTHS[:b]) for b in range(len(BANK_WIDTHS))]

        warm_in = pool.tile([P, 1], F32, name="warm_in")
        warm_out = pool.tile([P, 1], F32, name="warm_out")
        nc.gpsimd.memset(warm_in[:], 0.0)
        nc.scalar.activation(warm_out[:], warm_in[:], COPY)

        nc.vector.memset(tag_plane[:].bitcast(I32), 0)
        nc.vector.memset(key_plane[:].bitcast(I32), 0)
        nc.vector.memset(f1[:], 0.0)

        def load_query(j, src):
            nc.sync.dma_start(out=raw[j][:], in_=src.rearrange("(p r) q -> p r q", r=PACK))

        def load_plane(plane, scales):
            for r in range(4):
                nc.sync.dma_start(out=plane[r:P:32, :].bitcast(I32), in_=scales[0, r:16:4, :].bitcast(I32))

        load_query(1, query2)
        nc.sync.dma_start(out=tag_codes[:].bitcast(I32), in_=tags_words[0].bitcast(I32))
        load_plane(tag_plane, tags_scales)
        load_query(0, query)
        nc.sync.dma_start(out=key_codes[:].bitcast(I32),
                          in_=keys_words[0].rearrange("p n r -> p (n r)").bitcast(I32))
        load_plane(key_plane, keys_scales)
        nc.sync.dma_start(list_old[:], offs2)
        nc.sync.dma_start(list_a[:], offs)
        nc.sync.dma_start(out=old_sb[:], in_=old)
        nc.sync.dma_start(list_cc[:], offs3)
        nc.sync.dma_start(out=lam_sb[:], in_=lam)

        for j in (1, 0):
            nc.vector.tensor_copy(out=grouped[j][:], in_=raw[j][:].rearrange("p r q -> p q r"))
            nc.vector.quantize_mx(out=q_codes[j][:].bitcast(FP8X4), scales=q_plane[j][:],
                                  in_=grouped[j][:].rearrange("p q r -> p (q r)"))

        for bank, t0, n in zip(banks, starts, BANK_WIDTHS):
            nc.tensor.matmul_mx(out=bank[:], lhsT=q_codes[1][:].bitcast(FP8X4), lhsT_scale=q_plane[1][:],
                                rhs=tag_codes[:, 2 * t0:2 * (t0 + n)].bitcast(FP4X4),
                                rhs_scale=tag_plane[:, t0:t0 + n], start=True, stop=False)
        for b, (bank, t0, n) in enumerate(zip(banks, starts, BANK_WIDTHS)):
            nc.tensor.matmul_mx(out=bank[:], lhsT=q_codes[0][:].bitcast(FP8X4), lhsT_scale=q_plane[0][:],
                                rhs=key_codes[:, t0:t0 + n].bitcast(FP8X4),
                                rhs_scale=key_plane[:, t0:t0 + n], start=False, stop=True)
            if b % 2 == 0:
                nc.vector.tensor_copy(out=a_sb[:, t0:t0 + n], in_=bank[:])
            else:
                nc.scalar.copy(out=a_sb[:, t0:t0 + n], in_=bank[:])

        def half(lst, h):
            return lst[:, HALF_COLS * h:HALF_COLS * (h + 1)]

        nc.scalar.activation(a_pick[0][:], a_sb[:].indirect(half(list_a, 0)), COPY)
        nc.vector.tensor_scalar(old_neg[0][:], old_sb[:].indirect(half(list_old, 0)), -1.0, 0.0, MULT, ADD)
        nc.scalar.activation(a_pick[1][:], a_sb[:].indirect(half(list_a, 1)), COPY)
        nc.scalar.activation(old_neg[1][:], old_sb[:].indirect(half(list_old, 1)), COPY, scale=-1.0)
        for h in range(2):
            nc.vector.tensor_tensor(f1[:].indirect(half(list_old, h)), a_pick[h][:], old_neg[h][:], ADD)

        nc.vector.scalar_tensor_tensor(cc[:], f1[:], lam_sb[:], old_sb[:], MULT, ADD)

        nc.vector.tensor_copy(y[0][:], cc[:].indirect(half(list_cc, 0)))
        nc.scalar.activation(y[1][:], cc[:].indirect(half(list_cc, 1)), COPY)
        nc.sync.dma_start(out=out[:, 0:HALF_I], in_=y[0][:])
        nc.scalar.dma_start(out=out[:, HALF_I:I], in_=y[1][:])
